import numpy as np
import ml_dtypes


def mxq(x, axis, fmt="e4m3"):
    dtype, down = {"e4m3": (ml_dtypes.float8_e4m3fn, 7), "e5m2": (ml_dtypes.float8_e5m2, 14)}[fmt]
    v = np.moveaxis(np.asarray(x, np.float32).astype(ml_dtypes.bfloat16).astype(np.float64), axis, -1)
    blocks = v.reshape(v.shape[:-1] + (-1, 32))
    amax = np.abs(blocks).max(-1, keepdims=True)
    byte = np.maximum(np.where(amax > 0, np.frexp(amax)[1] - 1 + 127, 0) - down, 1)
    scale = np.exp2(byte - 127.0)
    codes = (blocks / scale).astype(np.float32).astype(dtype).astype(np.float64)
    return np.moveaxis((codes * scale).reshape(v.shape), -1, axis)


WIDE = False


def mx_kscale(k):
    if not WIDE:
        return np.ones(k)
    levels = np.array([10, -10, 5, -5, 0])
    if k % 512:
        return np.exp2(np.random.permutation(np.resize(levels, k // 32))).repeat(32)
    a = np.empty((k // 512, 16))
    for p in range(k // 512):
        a[p, :8] = np.random.permutation(np.resize(levels, 8))
        for g in range(8):
            far = levels[np.abs(levels - a[p, g]) >= 10]
            a[p, g + 8] = far[np.random.randint(len(far))]
    return np.exp2(a.ravel()).repeat(32)


BF16 = ml_dtypes.bfloat16


def bf(x):
    return np.asarray(x, np.float32).astype(BF16)


def f64(x):
    return np.asarray(x).astype(np.float64)


D, F, N = 4096, 512, 1024

ALPHA = 0.5


def draw0():
    s = mx_kscale(N)
    t = mx_kscale(N)
    c = 1.0 / np.sqrt(N)
    return {
        "w0": bf(np.random.standard_normal((D, F)) * 0.5),
        "coef": bf(np.random.standard_normal((N, N)) * c * s[None, :]),
        "g": bf((1.0 + 0.1 * np.random.standard_normal(N)) * t),
        "uc": bf(np.random.standard_normal((D, N)) * c / t[None, :]),
        "us": bf(np.random.standard_normal((D, N)) * c / t[None, :]),
        "vc": bf(np.random.standard_normal((N, F)) / s[:, None]),
        "vs": bf(np.random.standard_normal((N, F)) / s[:, None]),
    }


def core(w0, coef, g, uc, us, vc, vs):
    cq = mxq(f64(coef), 1, "e4m3")
    rc = cq @ mxq(f64(vc), 0, "e4m3")
    rs = cq @ mxq(f64(vs), 0, "e4m3")
    gain = f64(g)[:, None]
    zc = gain * rc
    zs = gain * rs
    pc = mxq(f64(uc), 1, "e4m3") @ mxq(zc, 0, "e4m3")
    ps = mxq(f64(us), 1, "e4m3") @ mxq(zs, 0, "e4m3")
    return f64(w0) + ALPHA * (pc - ps)


def e4m3fn_bytes(y):
    return np.clip(np.asarray(y, np.float64), -448.0, 448.0).astype(np.float32).astype(ml_dtypes.float8_e4m3fn).view(np.uint8)


def e4m3fn_values(b):
    return np.asarray(b, np.uint8).view(ml_dtypes.float8_e4m3fn).astype(np.float64)


def setup_inputs():
    d = draw0()
    x0 = np.asarray(d['us']).astype(np.float64)
    s = (np.max(np.abs(x0), axis=(0,), keepdims=True) / 448.0).astype(np.float32)
    out = {}
    for k, v in d.items():
        if k == 'us':
            out['us_bytes'] = e4m3fn_bytes(x0 / s.astype(np.float64))
            out['us_scale'] = s
        else:
            out[k] = v
    return out


def reference(w0, coef, g, uc, us_bytes, us_scale, vc, vs):
    return core(w0, coef, g, uc, e4m3fn_values(us_bytes) * us_scale.astype(np.float64), vc, vs)

from contextlib import ExitStack

import concourse.mybir as mybir
from concourse.masks import make_identity

D, F, N = 4096, 512, 1024
FLOPS = 2 * (2 * N * N * F) + 2 * (2 * D * N * F)

F32 = mybir.dt.float32
BF16 = mybir.dt.bfloat16
U32 = mybir.dt.uint32
U8 = mybir.dt.uint8
FP8 = mybir.dt.float8_e4m3fn
FP8X4 = mybir.dt.float8_e4m3fn_x4
ALU = mybir.AluOpType
ACT = mybir.ActivationFunctionType

P = 128
PASSES = N // 512
PAIRS = D // 256
T_AHEAD = 3


def tile_fourierftgivenbases_t_kernel(tc, w0, coef, g, uc, us_bytes, us_scale, vc, vs, out):
    nc = tc.nc
    coef_v = coef.rearrange("(g m t) j -> g m t j", m=P, t=4)
    v_views = [v.rearrange("(h p j) f -> h p j f", p=P, j=4) for v in (vc, vs)]
    uc_v = uc.rearrange("(q p s) k -> q p s k", p=P, s=4)
    us_v = us_bytes.rearrange("(q p s) k -> q p s k", p=P, s=4)
    w0_v = w0.rearrange("(q p s) f -> q p s f", p=P, s=4)
    out_v = out.rearrange("(q p s) f -> q p s f", p=P, s=4)

    with ExitStack() as ctx:
        def pool(name, bufs):
            return ctx.enter_context(tc.tile_pool(name=name, bufs=bufs))

        keep = pool("keep", 1)
        uc_pool = pool("ucp", 8)
        us_pool = pool("usp", 3)
        w0_pool = pool("w0p", 3)
        usb_pool = pool("usbp", 3)
        ucg_pool = pool("ucgp", 3)
        usg_pool = pool("usgp", 3)
        code_pool = pool("codep", 5)
        cg_pool = pool("cgp", 3)
        vi_pool = pool("vip", 2)
        zp_pool = pool("zpp", 3)
        zi_pool = pool("zip", 2)
        o_pool = pool("op", 2)
        tps = ctx.enter_context(tc.psum_pool(name="tps", bufs=4))
        aps = ctx.enter_context(tc.psum_pool(name="aps", bufs=4))
        ctx.enter_context(tc.manual_schedule())

        ident = keep.tile([P, P], F32, name="ident")
        make_identity(nc, ident[:])
        sc_rows = keep.tile([P, P], F32, name="sc_rows")
        nc.gpsimd.memset(sc_rows[:], 0.0)
        g_bf = keep.tile([P, PASSES, 4], BF16, name="g_bf")
        gain = keep.tile([P, 2, PASSES * 4], F32, name="gain")

        nc.sync.dma_start(out=sc_rows[0:8, :], in_=us_scale.rearrange("o (c q) -> (o c) q", q=P))
        coef_raw = [keep.tile([P, 4, N], BF16, name=f"coef_raw{gi}", align_bytes=64) for gi in range(PASSES)]
        v_raw = {}
        uc_t, us_t, w0_t = {}, {}, {}

        def load_coef(gi, t):
            nc.sync.dma_start(out=coef_raw[gi][:, t, :], in_=coef_v[gi][:, t, :])

        def load_v(b, h):
            raw = uc_pool.tile([P, 4, F], BF16, name="uc_raw", align_bytes=64)
            nc.sync.dma_start(out=raw[:], in_=v_views[b][h])
            v_raw[b, h] = raw

        def load_us(q, half=None):
            if q not in us_t:
                us_t[q] = us_pool.tile([P, 4, N], U8, name="us_raw", align_bytes=64)
            rows = slice(0, 4) if half is None else slice(2 * half, 2 * half + 2)
            nc.sync.dma_start(out=us_t[q][:, rows, :], in_=us_v[q][:, rows, :])

        def load_uc(i):
            q, r = divmod(i, 2)
            t = uc_pool.tile([P, 2, N], BF16, name="uc_raw", align_bytes=64)
            nc.sync.dma_start(out=t[:], in_=uc_v[q][:, 2 * r : 2 * r + 2, :])
            uc_t[i] = t

        def load_w0(q):
            t = w0_pool.tile([P, 4, F], BF16, name="w0_raw", align_bytes=64)
            nc.sync.dma_start(out=t[:], in_=w0_v[q])
            w0_t[q] = t

        load_coef(1, 0)
        load_coef(0, 0)
        load_coef(0, 1)
        load_us(0, 0)
        nc.sync.dma_start(out=g_bf[:], in_=g.rearrange("(g p t) -> p g t", p=P, t=4))
        load_v(0, 0)
        load_v(1, 1)
        load_coef(0, 2)

        nc.gpsimd.tensor_copy(out=gain[:, 0, :], in_=g_bf[:].rearrange("p g t -> p (g t)"))
        nc.gpsimd.tensor_scalar(
            out=gain[:, 1, :], in0=g_bf[:].rearrange("p g t -> p (g t)"), scalar1=-1.0, scalar2=None, op0=ALU.mult
        )

        scale = keep.tile([P, 2 * N], F32, name="scale", align_bytes=64)
        sc_cols = keep.tile([P, 8], F32, name="sc_cols")
        xt = tps.tile([P, 4, P], F32, name="xt")
        nc.tensor.transpose(xt[:, 0, :], sc_rows[:], ident[:])
        nc.vector.tensor_copy(out=sc_cols[:], in_=xt[:, 0, 0:8])
        for c0 in range(2):
            xt = tps.tile([P, 4, P], F32, name="xt")
            for c in range(4):
                col = sc_cols[:, 4 * c0 + c : 4 * c0 + c + 1]
                nc.tensor.transpose(xt[:, c, :], col.to_broadcast([P, P]), ident[:])
            bank = xt[:].rearrange("p c n -> p (c n)")
            nc.vector.tensor_copy(out=scale[:, c0 * 512 : (c0 + 1) * 512], in_=bank)
            nc.scalar.copy(out=scale[:, N + c0 * 512 : N + (c0 + 1) * 512], in_=bank)

        def turn(words, w_base, grouped, s):
            xt = tps.tile([P, 4, P], F32, name="xt")
            for gu in range(4):
                gi, u = divmod(gu, 2)
                lo = w_base + gi * 256 + u
                nc.tensor.transpose(xt[:, gu, :], words[:, lo : w_base + (gi + 1) * 256 : 2], ident[:])
            dst = grouped[:].bitcast(F32)[:, s * 512 : (s + 1) * 512]
            nc.scalar.copy(
                out=dst.rearrange("p (g d u) -> p g d u", g=2, u=2),
                in_=xt[:].rearrange("p (g u) d -> p g d u", u=2),
            )

        def quantize(src, codes, scales):
            nc.vector.quantize_mx(out=codes.bitcast(FP8X4), scales=scales, in_=src)

        coef_codes = keep.tile([P, 8, 2, P], U32, name="coef_codes", align_bytes=64)
        coef_sc = keep.tile([P, 8, 2, P], U8, name="coef_sc", align_bytes=64)
        v_codes = keep.tile([P, 4, F], U32, name="v_codes", align_bytes=64)
        v_sc = keep.tile([P, 4, F], U8, name="v_sc", align_bytes=64)
        z_codes = keep.tile([P, 4, F], U32, name="z_codes", align_bytes=64)
        z_sc = keep.tile([P, 4, F], U8, name="z_sc", align_bytes=64)
        coef_grp, v_grp, z_pl, z_grp = {}, {}, {}, {}

        def coef_turn(gi, a):
            grp = cg_pool.tile([P, 2048], BF16, name="coef_grp", align_bytes=64)
            words = coef_raw[gi][:].rearrange("p t j -> p (t j)").bitcast(F32)
            for s in range(2):
                turn(words, (2 * a + s) * 512, grp, s)
            coef_grp[gi, a] = grp

        def coef_quant(gi, a):
            lo = 4 * gi + 2 * a
            quantize(
                coef_grp[gi, a][:],
                coef_codes[:, lo : lo + 2].rearrange("p a h m -> p (a h m)"),
                coef_sc[:, lo : lo + 2].rearrange("p a h m -> p (a h m)"),
            )

        def interleave(engine, dst, src):
            if engine == "S":
                nc.scalar.copy(out=dst, in_=src)
            else:
                nc.vector.tensor_copy(out=dst, in_=src)

        def v_group(b, h, engine):
            grp = vi_pool.tile([P, F, 4], BF16, name="v_grp", align_bytes=64)
            interleave(engine, grp[:], v_raw[b, h][:].rearrange("p j f -> p f j"))
            v_grp[b, h] = grp

        def v_quant(b, h):
            quantize(v_grp[b, h][:].rearrange("p f j -> p (f j)"), v_codes[:, 2 * b + h, :], v_sc[:, 2 * b + h, :])

        def stage1(gi, b):
            planes = zp_pool.tile([P, 4, F], BF16, name="z_pl", align_bytes=64)
            for t in range(4):
                acc = aps.tile([P, F], F32, name="acc")
                for h in range(2):
                    nc.tensor.matmul_mx(
                        out=acc[:],
                        lhsT=coef_codes[:, 4 * gi + t, h, :].bitcast(FP8X4),
                        lhsT_scale=coef_sc[:, 4 * gi + t, h, :],
                        rhs=v_codes[:, 2 * b + h, :].bitcast(FP8X4),
                        rhs_scale=v_sc[:, 2 * b + h, :],
                        start=(h == 0),
                        stop=(h == 1),
                    )
                nc.scalar.activation(
                    out=planes[:, t, :], in_=acc[:], func=ACT.Copy, scale=gain[:, b, 4 * gi + t : 4 * gi + t + 1]
                )
            z_pl[gi, b] = planes

        def z_group(gi, b, engine):
            grp = zi_pool.tile([P, F, 4], BF16, name="z_grp", align_bytes=64)
            interleave(engine, grp[:], z_pl[gi, b][:].rearrange("p t f -> p f t"))
            z_grp[gi, b] = grp

        def z_quant(gi, b):
            quantize(z_grp[gi, b][:].rearrange("p f t -> p (f t)"), z_codes[:, 2 * b + gi, :], z_sc[:, 2 * b + gi, :])

        us_bf, u_grp, u_codes, accs = {}, {}, {}, {}

        def product(i):
            q, r = divmod(i, 2)
            t = usb_pool.tile([P, 2 * N], BF16, name="us_bf", align_bytes=64)
            nc.vector.tensor_tensor(
                out=t[:],
                in0=us_t[q][:, 2 * r : 2 * r + 2, :].rearrange("p s k -> p (s k)").bitcast(FP8),
                in1=scale[:],
                op=ALU.mult,
            )
            us_bf[i] = t

        def u_turn(i, b):
            if b == 0:
                grp = ucg_pool.tile([P, 2048], BF16, name="uc_grp", align_bytes=64)
                words = uc_t[i][:].rearrange("p s k -> p (s k)").bitcast(F32)
            else:
                grp = usg_pool.tile([P, 2048], BF16, name="us_grp", align_bytes=64)
                words = us_bf[i][:].bitcast(F32)
            for s in range(2):
                turn(words, s * 512, grp, s)
            u_grp[i, b] = grp

        def u_quant(i, b):
            codes = code_pool.tile([P, 4, P], U32, name=f"u_codes{b}", align_bytes=64)
            scales = code_pool.tile([P, 4, P], U8, name=f"u_sc{b}", align_bytes=64)
            quantize(u_grp[i, b][:], codes[:].rearrange("p a d -> p (a d)"), scales[:].rearrange("p a d -> p (a d)"))
            u_codes[i, b] = (codes, scales)

        def stage2(i, s):
            acc = aps.tile([P, F], F32, name="acc")
            for n in range(4):
                b, gi = divmod(n, 2)
                codes, scales = u_codes[i, b]
                nc.tensor.matmul_mx(
                    out=acc[:],
                    lhsT=codes[:, 2 * s + gi, :].bitcast(FP8X4),
                    lhsT_scale=scales[:, 2 * s + gi, :],
                    rhs=z_codes[:, n, :].bitcast(FP8X4),
                    rhs_scale=z_sc[:, n, :],
                    start=(n == 0),
                    stop=(n == 3),
                )
            accs[i, s] = acc

        outs = {}

        def finish(i, s):
            q, r = divmod(i, 2)
            if s == 0:
                outs[i] = o_pool.tile([P, 2, F], F32, name="o")
            nc.vector.scalar_tensor_tensor(
                out=outs[i][:, s, :], in0=accs[i, s][:], scalar=0.5, in1=w0_t[q][:, 2 * r + s, :],
                op0=ALU.mult, op1=ALU.add,
            )
            if i == PAIRS - 1:
                nc.sync.dma_start(out=out_v[q][:, 2 * r + s, :], in_=outs[i][:, s, :])
            elif s == 1:
                nc.sync.dma_start(out=out_v[q][:, 2 * r : 2 * r + 2, :], in_=outs[i][:])

        load_coef(0, 3)
        load_coef(1, 1)
        product(0)
        coef_turn(0, 0)
        v_group(0, 0, "S")
        coef_quant(0, 0)
        v_group(1, 1, "V")
        load_v(0, 1)
        load_uc(0)
        u_turn(0, 1)
        v_quant(0, 0)
        coef_turn(1, 0)
        v_quant(1, 1)
        coef_turn(0, 1)
        load_coef(1, 2)
        v_group(0, 1, "V")
        u_quant(0, 1)
        load_coef(1, 3)
        u_turn(0, 0)
        v_quant(0, 1)
        coef_quant(1, 0)
        load_v(1, 0)
        coef_turn(1, 1)
        load_us(0, 1)
        coef_quant(0, 1)
        v_group(1, 0, "V")
        load_uc(1)
        coef_quant(1, 1)
        load_us(1)
        u_quant(0, 0)
        v_quant(1, 0)
        load_uc(2)
        stage1(0, 0)
        stage1(1, 0)
        stage1(1, 1)
        z_group(0, 0, "V")
        load_uc(3)
        product(1)
        stage1(0, 1)
        load_w0(0)
        load_us(2)
        z_group(1, 0, "V")
        z_quant(0, 0)
        product(2)
        z_quant(1, 0)
        u_turn(1, 0)
        product(3)
        u_quant(1, 0)
        load_uc(4)
        load_uc(5)
        z_group(1, 1, "S")
        u_turn(2, 0)
        z_group(0, 1, "V")
        z_quant(1, 1)
        u_turn(1, 1)
        z_quant(0, 1)
        u_turn(2, 1)
        u_quant(1, 1)

        for k in range(PAIRS):
            if k + 6 < PAIRS:
                if k % 2 == 0:
                    load_us((k + 6) // 2)
                load_uc(k + 6)
            if k % 2 == 0 and k // 2 + 1 < PAIRS // 2:
                load_w0(k // 2 + 1)
            if k + T_AHEAD < PAIRS:
                u_turn(k + T_AHEAD, 0)
                u_turn(k + T_AHEAD, 1)
            if k > 0:
                finish(k - 1, 0)
            if k + 2 < PAIRS:
                u_quant(k + 2, 0)
            if k > 0:
                finish(k - 1, 1)
            if k + 2 < PAIRS:
                u_quant(k + 2, 1)
            if k + 4 < PAIRS:
                product(k + 4)
            stage2(k, 0)
            stage2(k, 1)
        finish(PAIRS - 1, 0)
        finish(PAIRS - 1, 1)
